import numpy as np
import ml_dtypes


def mxq(x, axis, fmt="e4m3"):
    dtype, down = {"e4m3": (ml_dtypes.float8_e4m3fn, 7), "e5m2": (ml_dtypes.float8_e5m2, 14)}[fmt]
    v = np.moveaxis(np.asarray(x, np.float32).astype(ml_dtypes.bfloat16).astype(np.float64), axis, -1)
    blocks = v.reshape(v.shape[:-1] + (-1, 32))
    amax = np.abs(blocks).max(-1, keepdims=True)
    byte = np.maximum(np.where(amax > 0, np.frexp(amax)[1] - 1 + 127, 0) - down, 1)
    scale = np.exp2(byte - 127.0)
    codes = (blocks / scale).astype(np.float32).astype(dtype).astype(np.float64)
    return np.moveaxis((codes * scale).reshape(v.shape), -1, axis)


WIDE = False


def mx_kscale(k):
    if not WIDE:
        return np.ones(k)
    levels = np.array([10, -10, 5, -5, 0])
    if k % 512:
        return np.exp2(np.random.permutation(np.resize(levels, k // 32))).repeat(32)
    a = np.empty((k // 512, 16))
    for p in range(k // 512):
        a[p, :8] = np.random.permutation(np.resize(levels, 8))
        for g in range(8):
            far = levels[np.abs(levels - a[p, g]) >= 10]
            a[p, g + 8] = far[np.random.randint(len(far))]
    return np.exp2(a.ravel()).repeat(32)


def f64(x):
    return np.asarray(x).astype(np.float64)


def striped(idx):
    return np.tile(np.asarray(idx).reshape(-1, 16).T, (8, 1)).astype(np.uint16)


def unstriped(offs):
    return offs[:16].T.reshape(-1).astype(np.int64)


E2M1 = np.array([0.0, 0.5, 1.0, 1.5, 2.0, 3.0, 4.0, 6.0, -0.0, -0.5, -1.0, -1.5, -2.0, -3.0, -4.0, -6.0])


def pack_weight(w, fmt):
    k, n = w.shape
    w = f64(np.asarray(w, np.float32).astype(ml_dtypes.bfloat16)).reshape(k // 32, 32, n)
    amax = np.abs(w).max(1)
    if fmt == "e4m3":
        byte = np.frexp(amax)[1] - 1 + 127 - 7
    else:
        mant, ex = np.frexp(amax / 6.0)
        byte = np.where(mant > 0.5, ex, ex - 1) + 127
    byte = np.clip(np.where(amax > 0, byte, 1), 1, 254)
    scaled = (w * np.exp2(127.0 - byte)[:, None, :]).reshape(k, n).astype(np.float32)
    by_word = np.ascontiguousarray(scaled.reshape(k // 512, 128, 4, n).transpose(0, 1, 3, 2))
    if fmt == "e4m3":
        words = by_word.astype(ml_dtypes.float8_e4m3fn).view(np.uint8)
    else:
        c = by_word.astype(ml_dtypes.float4_e2m1fn).view(np.uint8) & 0xF
        words = (c[..., 0::2] | (c[..., 1::2] << 4)).reshape(k // 512, 128, 2 * n)
    return np.ascontiguousarray(words), np.ascontiguousarray(byte.astype(np.uint8).reshape(k // 512, 16, n))


def unpack_weight(words, scales, fmt):
    g, _, n = scales.shape
    words = np.ascontiguousarray(words).reshape(g, 128, n, -1)
    if fmt == "e4m3":
        vals = words.view(ml_dtypes.float8_e4m3fn).astype(np.float64)
    else:
        nib = np.empty((g, 128, n, 4), np.uint8)
        nib[..., 0::2] = words & 0xF
        nib[..., 1::2] = words >> 4
        vals = E2M1[nib]
    vals = vals * np.repeat(np.exp2(scales.astype(np.float64) - 127.0), 8, axis=1)[..., None]
    return vals.transpose(0, 1, 3, 2).reshape(g * 512, n)


K, T, J, N, L, R = 512, 1024, 512, 512, 512, 512


def setup_inputs():
    n = np.random.standard_normal
    idx = np.random.permutation(T)[:J]
    fk = mx_kscale(K)
    fr = mx_kscale(R)
    fl = mx_kscale(L)
    xtp = pack_weight(n((K, T)) / fk[:, None], "e4m3")
    wap = pack_weight(n((K, R)) * 1 / np.sqrt(K) * fk[:, None] * fr, "e2m1")
    wbp = pack_weight(n((R, N)) * 1 / np.sqrt(R) / fr[:, None], "e4m3")
    sxp = pack_weight(n((L, J)) / fl[:, None], "e2m1")
    wcp = pack_weight(n((L, N)) * 1 / np.sqrt(L) * fl[:, None], "e4m3")
    return {
        "xt_words": xtp[0],
        "xt_scales": xtp[1],
        "wa_words": wap[0],
        "wa_scales": wap[1],
        "wb_words": wbp[0],
        "wb_scales": wbp[1],
        "sx_words": sxp[0],
        "sx_scales": sxp[1],
        "wc_words": wcp[0],
        "wc_scales": wcp[1],
        "ga": (np.random.uniform(0.4, 1.2, (1, J))).astype(np.float32),
        "offs": striped(idx),
    }


def reference(xt_words, xt_scales, wa_words, wa_scales, wb_words, wb_scales, sx_words, sx_scales, wc_words, wc_scales, ga, offs):
    idx = unstriped(offs)
    xtu = unpack_weight(xt_words, xt_scales, "e4m3")
    wau = unpack_weight(wa_words, wa_scales, "e2m1")
    wbu = unpack_weight(wb_words, wb_scales, "e4m3")
    sxu = unpack_weight(sx_words, sx_scales, "e2m1")
    wcu = unpack_weight(wc_words, wc_scales, "e4m3")
    xtidxg = xtu[:, idx]
    a = wau.T @ xtidxg
    hid = np.maximum(a, 0.0)
    hidq = mxq(hid, 0, "e4m3")
    p = wbu.T @ hidq + wcu.T @ sxu
    pw = p * f64(ga)
    y = np.zeros((N, T))
    y[:, idx] = pw
    return y

@@ -1,0 +1,197 @@
+from contextlib import ExitStack
+
+import concourse.mybir as mybir
+from concourse.masks import make_identity
+
+K, T, J, N, L, R = 512, 1024, 512, 512, 512, 512
+FLOPS = 2 * J * (K * R + R * N + L * N)
+
+F32 = mybir.dt.float32
+BF16 = mybir.dt.bfloat16
+I32 = mybir.dt.int32
+U32 = mybir.dt.uint32
+U16 = mybir.dt.uint16
+U8 = mybir.dt.uint8
+FP8X4 = mybir.dt.float8_e4m3fn_x4
+FP4X4 = mybir.dt.float4_e2m1fn_x4
+RELU = mybir.ActivationFunctionType.Relu
+COPY = mybir.ActivationFunctionType.Copy
+MULT = mybir.AluOpType.mult
+
+P = 128
+PACK = 4
+PIECE = 128
+PIECES = J // PIECE
+N_TILES = N // P
+LIST_ROWS = 16
+
+
+def load_scale_rows(queue, plane, scales, rows=range(4)):
+    for b in rows:
+        queue.dma_start(out=plane[b:P:32, :].bitcast(I32), in_=scales[0, b:16:4, :].bitcast(I32))
+
+
+def tile_moe_expert_hidden_and_given_kernel(
+    tc, xt_words, xt_scales, wa_words, wa_scales, wb_words, wb_scales, sx_words, sx_scales, wc_words, wc_scales, ga, offs, out
+):
+    nc = tc.nc
+
+    def listed(window, first, count):
+        return window.indirect(offsets[:, first // LIST_ROWS : (first + count) // LIST_ROWS])
+
+    with ExitStack() as ctx:
+        keep = ctx.enter_context(tc.tile_pool(name="keep", bufs=1))
+        psum = ctx.enter_context(tc.psum_pool(name="psum", bufs=1))
+
+        offsets = keep.tile([P, J // LIST_ROWS], U16, name="offsets")
+        ga_cols = keep.tile([P, PACK], F32, name="ga_cols")
+        wa_raw = keep.tile([P, 2 * R], U8, name="wa_raw", align_bytes=64)
+        wa_raw_scale = keep.tile([P, R], U8, name="wa_raw_scale", tag="wa_raw_scale", align_bytes=64)
+        xt_w = keep.tile([P, T], I32, name="xt_w", tag="xt_w", align_bytes=64)
+        xt_s = keep.tile([P, T], U8, name="xt_s", align_bytes=64)
+        late_s = keep.tile([P, 3 * 512], U8, name="late_s", align_bytes=64)
+        wb_s, wc_s, sx_s = late_s[:, 0:512], late_s[:, 512:1024], late_s[:, 1024:1536]
+        windows = [keep.tile([P, T], F32, name=f"window{n}") for n in range(2)]
+
+        nc.vector.memset(xt_s[:].bitcast(I32), 0)
+        nc.vector.memset(wa_raw_scale[:].bitcast(I32), 0)
+        nc.vector.memset(late_s[:].bitcast(I32), 0)
+        load_scale_rows(nc.scalar, xt_s, xt_scales)
+        load_scale_rows(nc.scalar, wa_raw_scale, wa_scales, (0, 1))
+        nc.sync.dma_start(offsets[:], offs)
+        nc.sync.dma_start(out=ga_cols[:], in_=ga.rearrange("o (p c) -> (o p) c", c=PACK))
+        nc.sync.dma_start(out=wa_raw[:].bitcast(I32), in_=wa_words[0].bitcast(I32))
+        nc.sync.dma_start(out=xt_w[:], in_=xt_words[0].rearrange("p n t -> p (n t)").bitcast(I32))
+        load_scale_rows(nc.sync, wa_raw_scale, wa_scales, (2, 3))
+
+        late_w = keep.tile([P, 1280], I32, name="late_w", align_bytes=64)
+        wb_w, wc_w, sx_w = late_w[:, 0:512], late_w[:, 512:1024], late_w[:, 1024:1280]
+        load_scale_rows(nc.sync, sx_s, sx_scales)
+        load_scale_rows(nc.sync, wc_s, wc_scales, (0, 1, 2))
+        nc.sync.dma_start(out=sx_w, in_=sx_words[0].bitcast(I32))
+        nc.sync.dma_start(out=wc_w, in_=wc_words[0].rearrange("p n t -> p (n t)").bitcast(I32))
+        nc.sync.dma_start(out=wb_w, in_=wb_words[0].rearrange("p n t -> p (n t)").bitcast(I32))
+        load_scale_rows(nc.sync, wc_s, wc_scales, (3,))
+        load_scale_rows(nc.sync, wb_s, wb_scales)
+
+        for n in range(2):
+            nc.vector.memset(windows[n][:].bitcast(I32), 0)
+
+        ident = keep.tile([P, P], F32, name="ident", tag="ident", align_bytes=64)
+        make_identity(nc, ident[:])
+        gate_ps = psum.tile([P, PACK, P], F32, name="gate_ps", tag="bank0")
+        for c in range(PACK):
+            nc.tensor.transpose(gate_ps[:, c, :], ga_cols[:, c : c + 1].to_broadcast([P, P]), ident[:])
+        gate = keep.tile([P, J], F32, name="gate")
+        nc.scalar.activation(out=gate[:].rearrange("p (m c) -> p m c", c=PACK), in_=gate_ps[:].rearrange("p c m -> p m c"), func=COPY)
+
+        wa_w = keep.tile([P, 2 * R], U8, name="wa_w", align_bytes=64)
+        wa_s = keep.tile([P, R], U8, name="wa_s", tag="ident", align_bytes=64)
+        nc.vector.tensor_copy(
+            out=wa_w[:].bitcast(U16).rearrange("p (t m) -> p t m", t=PACK),
+            in_=wa_raw[:].bitcast(U16).rearrange("p (m t) -> p t m", t=PACK),
+        )
+
+        def permute_scales():
+            nc.vector.tensor_copy(
+                out=wa_s[:].rearrange("p (t m) -> p t m", t=PACK),
+                in_=wa_raw_scale[:].rearrange("p (m t) -> p t m", t=PACK),
+            )
+
+        xg_s = keep.tile([P, J], U8, name="xg_s", align_bytes=64)
+        nc.vector.tensor_copy(xg_s[:], listed(xt_s[:], 0, J))
+        xg_lead = keep.tile([P, PIECE], U32, name="xg_lead", align_bytes=64)
+        nc.vector.tensor_copy(xg_lead[:], listed(xt_w[:].bitcast(U32), 0, PIECE))
+        permute_scales()
+        xg_rest = keep.tile([P, J - PIECE], U32, name="xg_rest", tag="wa_raw_scale", align_bytes=64)
+        xg_w = [xg_lead[:]] + [xg_rest[:, i * PIECE : (i + 1) * PIECE] for i in range(PIECES - 1)]
+
+        hid = [keep.tile([P, PIECE, PACK], BF16, name=f"hid{i}", tag=f"hid{i}", align_bytes=64) for i in range(PIECES)]
+        hid_w = [keep.tile([P, PIECE], U32, name=f"hid_w{i}", align_bytes=64) for i in range(PIECES)]
+        hid_s = [keep.tile([P, PIECE], U8, name=f"hid_s{i}", align_bytes=64) for i in range(PIECES)]
+        a_ps = {}
+
+        def first_layer(i):
+            a_ps[i] = psum.tile([P, PACK, PIECE], F32, name=f"a_ps{i}", tag=f"bank{1 + i}")
+            cols = slice(i * PIECE, (i + 1) * PIECE)
+            for t in range(PACK):
+                nc.tensor.matmul_mx(
+                    out=a_ps[i][:, t, :],
+                    lhsT=wa_w[:, 2 * P * t : 2 * P * (t + 1)].bitcast(FP4X4),
+                    lhsT_scale=wa_s[:, P * t : P * (t + 1)],
+                    rhs=xg_w[i].bitcast(FP8X4),
+                    rhs_scale=xg_s[:, cols],
+                    start=True,
+                    stop=True,
+                )
+
+        def relu(i):
+            nc.scalar.activation(out=hid[i][:], in_=a_ps[i][:].rearrange("p t j -> p j t"), func=RELU)
+
+        def quantize(i):
+            nc.vector.quantize_mx(out=hid_w[i][:].bitcast(FP8X4), scales=hid_s[i][:], in_=hid[i][:].rearrange("p j t -> p (j t)"))
+
+        def second_layer(dst, n, i):
+            rows = slice(n * P, (n + 1) * P)
+            cols = slice(i * PIECE, (i + 1) * PIECE)
+            nc.tensor.matmul_mx(
+                out=dst,
+                lhsT=wc_w[:, rows].bitcast(FP8X4),
+                lhsT_scale=wc_s[:, rows],
+                rhs=sx_w[:, i * PIECE // 2 : (i + 1) * PIECE // 2].bitcast(FP4X4),
+                rhs_scale=sx_s[:, cols],
+                start=True,
+                stop=False,
+            )
+            nc.tensor.matmul_mx(
+                out=dst,
+                lhsT=wb_w[:, rows].bitcast(FP8X4),
+                lhsT_scale=wb_s[:, rows],
+                rhs=hid_w[i][:].bitcast(FP8X4),
+                rhs_scale=hid_s[i][:],
+                start=False,
+                stop=True,
+            )
+
+        def scatter(n, first, count, src):
+            nc.vector.tensor_tensor(listed(windows[n][:], first, count), src, gate[:, first : first + count], MULT)
+
+        first_layer(0)
+        nc.vector.tensor_copy(xg_rest[:], listed(xt_w[:].bitcast(U32), PIECE, J - PIECE))
+        windows.append(keep.tile([P, T], F32, name="window2", tag="xt_w", align_bytes=64))
+        nc.vector.memset(windows[2][:].bitcast(I32), 0)
+        relu(0)
+        quantize(0)
+        windows.append(keep.tile([P, T], F32, name="window3", tag="hid0", align_bytes=64))
+        nc.vector.memset(windows[3][:].bitcast(I32), 0)
+        first_layer(1)
+
+        lead_ps = [psum.tile([P, 2, PIECE], F32, name=f"lead_ps{h}", tag=f"bank{5 + h}") for h in range(2)]
+        lead = [keep.tile([P, PIECE], F32, name=f"lead{n}") for n in range(N_TILES)]
+        second_layer(lead_ps[0][:, 0, :], 0, 0)
+        second_layer(lead_ps[1][:, 0, :], 1, 0)
+        relu(1)
+        quantize(1)
+        for n in range(2):
+            nc.scalar.copy(out=lead[n][:], in_=lead_ps[n][:, 0, :])
+            scatter(n, 0, PIECE, lead[n][:])
+        first_layer(2)
+        first_layer(3)
+        second_layer(lead_ps[0][:, 1, :], 2, 0)
+        second_layer(lead_ps[1][:, 1, :], 3, 0)
+        for i in (2, 3):
+            relu(i)
+            quantize(i)
+        for n in range(2, N_TILES):
+            nc.scalar.copy(out=lead[n][:], in_=lead_ps[n - 2][:, 1, :])
+            scatter(n, 0, PIECE, lead[n][:])
+
+        rest_banks = [7, 0, 1, 2]
+        for n in range(N_TILES):
+            rest_ps = psum.tile([P, PIECES - 1, PIECE], F32, name=f"rest_ps{n}", tag=f"bank{rest_banks[n]}")
+            for i in range(1, PIECES):
+                second_layer(rest_ps[:, i - 1, :], n, i)
+            rest = keep.tile([P, J - PIECE], F32, name=f"rest{n}")
+            nc.scalar.copy(out=rest[:], in_=rest_ps[:].rearrange("p i j -> p (i j)"))
+            scatter(n, PIECE, J - PIECE, rest[:])
+            nc.sync.dma_start(out=out[n * P : (n + 1) * P, :], in_=windows[n][:])

@@ -44,14 +44,14 @@ def tile_moe_expert_hidden_and_given_kernel(
         psum = ctx.enter_context(tc.psum_pool(name="psum", bufs=1))
 
         offsets = keep.tile([P, J // LIST_ROWS], U16, name="offsets")
-        ga_cols = keep.tile([P, PACK], F32, name="ga_cols")
+        ga_cols = keep.tile([P, PACK], F32, name="ga_cols", tag="ga_cols", align_bytes=64)
         wa_raw = keep.tile([P, 2 * R], U8, name="wa_raw", align_bytes=64)
         wa_raw_scale = keep.tile([P, R], U8, name="wa_raw_scale", tag="wa_raw_scale", align_bytes=64)
         xt_w = keep.tile([P, T], I32, name="xt_w", tag="xt_w", align_bytes=64)
         xt_s = keep.tile([P, T], U8, name="xt_s", align_bytes=64)
         late_s = keep.tile([P, 3 * 512], U8, name="late_s", align_bytes=64)
         wb_s, wc_s, sx_s = late_s[:, 0:512], late_s[:, 512:1024], late_s[:, 1024:1536]
-        windows = [keep.tile([P, T], F32, name=f"window{n}") for n in range(2)]
+        windows = [keep.tile([P, T], F32, name=f"window{n}") for n in range(3)]
 
         nc.vector.memset(xt_s[:].bitcast(I32), 0)
         nc.vector.memset(wa_raw_scale[:].bitcast(I32), 0)
@@ -66,15 +66,14 @@ def tile_moe_expert_hidden_and_given_kernel(
 
         late_w = keep.tile([P, 1280], I32, name="late_w", align_bytes=64)
         wb_w, wc_w, sx_w = late_w[:, 0:512], late_w[:, 512:1024], late_w[:, 1024:1280]
-        load_scale_rows(nc.sync, sx_s, sx_scales)
-        load_scale_rows(nc.sync, wc_s, wc_scales, (0, 1, 2))
         nc.sync.dma_start(out=sx_w, in_=sx_words[0].bitcast(I32))
         nc.sync.dma_start(out=wc_w, in_=wc_words[0].rearrange("p n t -> p (n t)").bitcast(I32))
         nc.sync.dma_start(out=wb_w, in_=wb_words[0].rearrange("p n t -> p (n t)").bitcast(I32))
-        load_scale_rows(nc.sync, wc_s, wc_scales, (3,))
+        load_scale_rows(nc.sync, sx_s, sx_scales)
+        load_scale_rows(nc.sync, wc_s, wc_scales)
         load_scale_rows(nc.sync, wb_s, wb_scales)
 
-        for n in range(2):
+        for n in range(3):
             nc.vector.memset(windows[n][:].bitcast(I32), 0)
 
         ident = keep.tile([P, P], F32, name="ident", tag="ident", align_bytes=64)
@@ -98,29 +97,36 @@ def tile_moe_expert_hidden_and_given_kernel(
                 in_=wa_raw_scale[:].rearrange("p (m t) -> p t m", t=PACK),
             )
 
-        xg_s = keep.tile([P, J], U8, name="xg_s", align_bytes=64)
-        nc.vector.tensor_copy(xg_s[:], listed(xt_s[:], 0, J))
-        xg_lead = keep.tile([P, PIECE], U32, name="xg_lead", align_bytes=64)
-        nc.vector.tensor_copy(xg_lead[:], listed(xt_w[:].bitcast(U32), 0, PIECE))
+        def gather_words(dst, first, count):
+            nc.vector.tensor_copy(dst, listed(xt_w[:].bitcast(U32), first, count))
+
+        def gather_scales(dst, first, count):
+            nc.vector.tensor_copy(dst, listed(xt_s[:], first, count))
+
+        xg_s0 = keep.tile([P, PIECE], U8, name="xg_s0", align_bytes=64)
+        xg_w0 = keep.tile([P, PIECE], U32, name="xg_w0", align_bytes=64)
+        gather_scales(xg_s0[:], 0, PIECE)
+        gather_words(xg_w0[:], 0, PIECE)
         permute_scales()
-        xg_rest = keep.tile([P, J - PIECE], U32, name="xg_rest", tag="wa_raw_scale", align_bytes=64)
-        xg_w = [xg_lead[:]] + [xg_rest[:, i * PIECE : (i + 1) * PIECE] for i in range(PIECES - 1)]
+        xg_w1 = keep.tile([P, PIECE], U32, name="xg_w1", tag="wa_raw_scale", align_bytes=64)
+        xg_s123 = keep.tile([P, J - PIECE], U8, name="xg_s123", tag="ga_cols", align_bytes=64)
+        xg_w = {0: xg_w0[:], 1: xg_w1[:]}
+        xg_s = [xg_s0[:]] + [xg_s123[:, i * PIECE : (i + 1) * PIECE] for i in range(PIECES - 1)]
 
         hid = [keep.tile([P, PIECE, PACK], BF16, name=f"hid{i}", tag=f"hid{i}", align_bytes=64) for i in range(PIECES)]
         hid_w = [keep.tile([P, PIECE], U32, name=f"hid_w{i}", align_bytes=64) for i in range(PIECES)]
         hid_s = [keep.tile([P, PIECE], U8, name=f"hid_s{i}", align_bytes=64) for i in range(PIECES)]
         a_ps = {}
 
-        def first_layer(i):
-            a_ps[i] = psum.tile([P, PACK, PIECE], F32, name=f"a_ps{i}", tag=f"bank{1 + i}")
-            cols = slice(i * PIECE, (i + 1) * PIECE)
+        def first_layer(i, bank):
+            a_ps[i] = psum.tile([P, PACK, PIECE], F32, name=f"a_ps{i}", tag=f"bank{bank}")
             for t in range(PACK):
                 nc.tensor.matmul_mx(
                     out=a_ps[i][:, t, :],
                     lhsT=wa_w[:, 2 * P * t : 2 * P * (t + 1)].bitcast(FP4X4),
                     lhsT_scale=wa_s[:, P * t : P * (t + 1)],
                     rhs=xg_w[i].bitcast(FP8X4),
-                    rhs_scale=xg_s[:, cols],
+                    rhs_scale=xg_s[i],
                     start=True,
                     stop=True,
                 )
@@ -156,37 +162,47 @@ def tile_moe_expert_hidden_and_given_kernel(
         def scatter(n, first, count, src):
             nc.vector.tensor_tensor(listed(windows[n][:], first, count), src, gate[:, first : first + count], MULT)
 
-        first_layer(0)
-        nc.vector.tensor_copy(xg_rest[:], listed(xt_w[:].bitcast(U32), PIECE, J - PIECE))
-        windows.append(keep.tile([P, T], F32, name="window2", tag="xt_w", align_bytes=64))
-        nc.vector.memset(windows[2][:].bitcast(I32), 0)
+        lead = [keep.tile([P, PIECE], F32, name=f"lead{n}") for n in range(N_TILES)]
+        lead_ps = {}
+
+        def lead_product(n):
+            lead_ps[n] = psum.tile([P, PIECE], F32, name=f"lead_ps{n}", tag=f"bank{3 + n % 2}")
+            second_layer(lead_ps[n][:], n, 0)
+
+        def lead_scatter(n):
+            nc.scalar.copy(out=lead[n][:], in_=lead_ps[n][:])
+            scatter(n, 0, PIECE, lead[n][:])
+
+        first_layer(0, 1)
+        gather_words(xg_w1[:], PIECE, PIECE)
+        gather_scales(xg_s123[:, 0:PIECE], PIECE, PIECE)
+        first_layer(1, 2)
+        gather_scales(xg_s123[:, PIECE:], 2 * PIECE, 2 * PIECE)
         relu(0)
         quantize(0)
-        windows.append(keep.tile([P, T], F32, name="window3", tag="hid0", align_bytes=64))
-        nc.vector.memset(windows[3][:].bitcast(I32), 0)
-        first_layer(1)
-
-        lead_ps = [psum.tile([P, 2, PIECE], F32, name=f"lead_ps{h}", tag=f"bank{5 + h}") for h in range(2)]
-        lead = [keep.tile([P, PIECE], F32, name=f"lead{n}") for n in range(N_TILES)]
-        second_layer(lead_ps[0][:, 0, :], 0, 0)
-        second_layer(lead_ps[1][:, 0, :], 1, 0)
+        xg_w23 = keep.tile([P, 2 * PIECE], U32, name="xg_w23", tag="hid0", align_bytes=64)
+        xg_w[2], xg_w[3] = xg_w23[:, 0:PIECE], xg_w23[:, PIECE:]
+        gather_words(xg_w23[:], 2 * PIECE, 2 * PIECE)
         relu(1)
         quantize(1)
-        for n in range(2):
-            nc.scalar.copy(out=lead[n][:], in_=lead_ps[n][:, 0, :])
-            scatter(n, 0, PIECE, lead[n][:])
-        first_layer(2)
-        first_layer(3)
-        second_layer(lead_ps[0][:, 1, :], 2, 0)
-        second_layer(lead_ps[1][:, 1, :], 3, 0)
+        windows.append(keep.tile([P, T], F32, name="window3", tag="xt_w", align_bytes=64))
+        nc.vector.memset(windows[3][:].bitcast(I32), 0)
+
+        for n in (0, 1):
+            lead_product(n)
+        for n in (0, 1):
+            lead_scatter(n)
+        for i in (2, 3):
+            first_layer(i, 1 + i)
         for i in (2, 3):
             relu(i)
             quantize(i)
-        for n in range(2, N_TILES):
-            nc.scalar.copy(out=lead[n][:], in_=lead_ps[n - 2][:, 1, :])
-            scatter(n, 0, PIECE, lead[n][:])
+        for n in (2, 3):
+            lead_product(n)
+        for n in (2, 3):
+            lead_scatter(n)
 
-        rest_banks = [7, 0, 1, 2]
+        rest_banks = [5, 3, 4, 5]
         for n in range(N_TILES):
             rest_ps = psum.tile([P, PIECES - 1, PIECE], F32, name=f"rest_ps{n}", tag=f"bank{rest_banks[n]}")
             for i in range(1, PIECES):

@@ -51,33 +51,35 @@ def tile_moe_expert_hidden_and_given_kernel(
         xt_s = keep.tile([P, T], U8, name="xt_s", align_bytes=64)
         late_s = keep.tile([P, 3 * 512], U8, name="late_s", align_bytes=64)
         wb_s, wc_s, sx_s = late_s[:, 0:512], late_s[:, 512:1024], late_s[:, 1024:1536]
+        ident = keep.tile([P, P], F32, name="ident", tag="ident", align_bytes=64)
+        make_identity(nc, ident[:])
         windows = [keep.tile([P, T], F32, name=f"window{n}") for n in range(3)]
 
         nc.vector.memset(xt_s[:].bitcast(I32), 0)
         nc.vector.memset(wa_raw_scale[:].bitcast(I32), 0)
         nc.vector.memset(late_s[:].bitcast(I32), 0)
-        load_scale_rows(nc.scalar, xt_s, xt_scales)
-        load_scale_rows(nc.scalar, wa_raw_scale, wa_scales, (0, 1))
         nc.sync.dma_start(offsets[:], offs)
-        nc.sync.dma_start(out=ga_cols[:], in_=ga.rearrange("o (p c) -> (o p) c", c=PACK))
-        nc.sync.dma_start(out=wa_raw[:].bitcast(I32), in_=wa_words[0].bitcast(I32))
+        nc.scalar.dma_start(out=wa_raw[:].bitcast(I32), in_=wa_words[0].bitcast(I32))
+        nc.scalar.dma_start(out=ga_cols[:], in_=ga.rearrange("o (p c) -> (o p) c", c=PACK))
+        load_scale_rows(nc.sync, xt_s, xt_scales, (0, 1))
+        load_scale_rows(nc.scalar, xt_s, xt_scales, (2, 3))
         nc.sync.dma_start(out=xt_w[:], in_=xt_words[0].rearrange("p n t -> p (n t)").bitcast(I32))
+        load_scale_rows(nc.scalar, wa_raw_scale, wa_scales, (0, 1))
         load_scale_rows(nc.sync, wa_raw_scale, wa_scales, (2, 3))
 
         late_w = keep.tile([P, 1280], I32, name="late_w", align_bytes=64)
         wb_w, wc_w, sx_w = late_w[:, 0:512], late_w[:, 512:1024], late_w[:, 1024:1280]
+        load_scale_rows(nc.gpsimd, wb_s, wb_scales)
         nc.sync.dma_start(out=sx_w, in_=sx_words[0].bitcast(I32))
         nc.sync.dma_start(out=wc_w, in_=wc_words[0].rearrange("p n t -> p (n t)").bitcast(I32))
+        load_scale_rows(nc.sync, sx_s, sx_scales, (0,))
         nc.sync.dma_start(out=wb_w, in_=wb_words[0].rearrange("p n t -> p (n t)").bitcast(I32))
-        load_scale_rows(nc.sync, sx_s, sx_scales)
+        load_scale_rows(nc.sync, sx_s, sx_scales, (1, 2, 3))
         load_scale_rows(nc.sync, wc_s, wc_scales)
-        load_scale_rows(nc.sync, wb_s, wb_scales)
 
         for n in range(3):
             nc.vector.memset(windows[n][:].bitcast(I32), 0)
 
-        ident = keep.tile([P, P], F32, name="ident", tag="ident", align_bytes=64)
-        make_identity(nc, ident[:])
         gate_ps = psum.tile([P, PACK, P], F32, name="gate_ps", tag="bank0")
         for c in range(PACK):
             nc.tensor.transpose(gate_ps[:, c, :], ga_cols[:, c : c + 1].to_broadcast([P, P]), ident[:])
@@ -108,14 +110,14 @@ def tile_moe_expert_hidden_and_given_kernel(
         gather_scales(xg_s0[:], 0, PIECE)
         gather_words(xg_w0[:], 0, PIECE)
         permute_scales()
-        xg_w1 = keep.tile([P, PIECE], U32, name="xg_w1", tag="wa_raw_scale", align_bytes=64)
+        xg_w123 = keep.tile([P, J - PIECE], U32, name="xg_w123", tag="wa_raw_scale", align_bytes=64)
         xg_s123 = keep.tile([P, J - PIECE], U8, name="xg_s123", tag="ga_cols", align_bytes=64)
-        xg_w = {0: xg_w0[:], 1: xg_w1[:]}
+        xg_w = [xg_w0[:]] + [xg_w123[:, i * PIECE : (i + 1) * PIECE] for i in range(PIECES - 1)]
         xg_s = [xg_s0[:]] + [xg_s123[:, i * PIECE : (i + 1) * PIECE] for i in range(PIECES - 1)]
 
         hid = [keep.tile([P, PIECE, PACK], BF16, name=f"hid{i}", tag=f"hid{i}", align_bytes=64) for i in range(PIECES)]
-        hid_w = [keep.tile([P, PIECE], U32, name=f"hid_w{i}", align_bytes=64) for i in range(PIECES)]
-        hid_s = [keep.tile([P, PIECE], U8, name=f"hid_s{i}", align_bytes=64) for i in range(PIECES)]
+        hid_w = keep.tile([P, J], U32, name="hid_w", align_bytes=64)
+        hid_s = keep.tile([P, J], U8, name="hid_s", align_bytes=64)
         a_ps = {}
 
         def first_layer(i, bank):
@@ -135,16 +137,17 @@ def tile_moe_expert_hidden_and_given_kernel(
             nc.scalar.activation(out=hid[i][:], in_=a_ps[i][:].rearrange("p t j -> p j t"), func=RELU)
 
         def quantize(i):
-            nc.vector.quantize_mx(out=hid_w[i][:].bitcast(FP8X4), scales=hid_s[i][:], in_=hid[i][:].rearrange("p j t -> p (j t)"))
-
-        def second_layer(dst, n, i):
-            rows = slice(n * P, (n + 1) * P)
             cols = slice(i * PIECE, (i + 1) * PIECE)
+            nc.vector.quantize_mx(out=hid_w[:, cols].bitcast(FP8X4), scales=hid_s[:, cols], in_=hid[i][:].rearrange("p j t -> p (j t)"))
+
+        def second_layer(dst, n, first, count):
+            rows = slice(n * P, (n + 1) * P)
+            cols = slice(first, first + count)
             nc.tensor.matmul_mx(
                 out=dst,
                 lhsT=wc_w[:, rows].bitcast(FP8X4),
                 lhsT_scale=wc_s[:, rows],
-                rhs=sx_w[:, i * PIECE // 2 : (i + 1) * PIECE // 2].bitcast(FP4X4),
+                rhs=sx_w[:, first // 2 : (first + count) // 2].bitcast(FP4X4),
                 rhs_scale=sx_s[:, cols],
                 start=True,
                 stop=False,
@@ -153,8 +156,8 @@ def tile_moe_expert_hidden_and_given_kernel(
                 out=dst,
                 lhsT=wb_w[:, rows].bitcast(FP8X4),
                 lhsT_scale=wb_s[:, rows],
-                rhs=hid_w[i][:].bitcast(FP8X4),
-                rhs_scale=hid_s[i][:],
+                rhs=hid_w[:, cols].bitcast(FP8X4),
+                rhs_scale=hid_s[:, cols],
                 start=False,
                 stop=True,
             )
@@ -162,52 +165,31 @@ def tile_moe_expert_hidden_and_given_kernel(
         def scatter(n, first, count, src):
             nc.vector.tensor_tensor(listed(windows[n][:], first, count), src, gate[:, first : first + count], MULT)
 
-        lead = [keep.tile([P, PIECE], F32, name=f"lead{n}") for n in range(N_TILES)]
-        lead_ps = {}
-
-        def lead_product(n):
-            lead_ps[n] = psum.tile([P, PIECE], F32, name=f"lead_ps{n}", tag=f"bank{3 + n % 2}")
-            second_layer(lead_ps[n][:], n, 0)
-
-        def lead_scatter(n):
-            nc.scalar.copy(out=lead[n][:], in_=lead_ps[n][:])
-            scatter(n, 0, PIECE, lead[n][:])
+        def result(n, first, count, step, bank):
+            p_ps = psum.tile([P, count], F32, name=f"p_ps{n}_{first}", tag=f"bank{bank}")
+            for j in range(0, count, step):
+                second_layer(p_ps[:, j : j + step], n, first + j, step)
+            p_sb = keep.tile([P, count], F32, name=f"p_sb{n}_{first}")
+            nc.scalar.copy(out=p_sb[:], in_=p_ps[:])
+            scatter(n, first, count, p_sb[:])
+            return p_sb
 
         first_layer(0, 1)
-        gather_words(xg_w1[:], PIECE, PIECE)
-        gather_scales(xg_s123[:, 0:PIECE], PIECE, PIECE)
-        first_layer(1, 2)
-        gather_scales(xg_s123[:, PIECE:], 2 * PIECE, 2 * PIECE)
-        relu(0)
-        quantize(0)
-        xg_w23 = keep.tile([P, 2 * PIECE], U32, name="xg_w23", tag="hid0", align_bytes=64)
-        xg_w[2], xg_w[3] = xg_w23[:, 0:PIECE], xg_w23[:, PIECE:]
-        gather_words(xg_w23[:], 2 * PIECE, 2 * PIECE)
-        relu(1)
-        quantize(1)
+        for i in range(1, PIECES):
+            gather_words(xg_w[i], i * PIECE, PIECE)
+            gather_scales(xg_s[i], i * PIECE, PIECE)
+            first_layer(i, 1 + i)
+        for i in range(PIECES):
+            relu(i)
+            quantize(i)
         windows.append(keep.tile([P, T], F32, name="window3", tag="xt_w", align_bytes=64))
         nc.vector.memset(windows[3][:].bitcast(I32), 0)
 
-        for n in (0, 1):
-            lead_product(n)
-        for n in (0, 1):
-            lead_scatter(n)
-        for i in (2, 3):
-            first_layer(i, 1 + i)
-        for i in (2, 3):
-            relu(i)
-            quantize(i)
-        for n in (2, 3):
-            lead_product(n)
-        for n in (2, 3):
-            lead_scatter(n)
-
-        rest_banks = [5, 3, 4, 5]
+        lead0 = result(0, 0, PIECE, PIECE, 5)
+        result(1, 0, PIECE, PIECE, 6)
         for n in range(N_TILES):
-            rest_ps = psum.tile([P, PIECES - 1, PIECE], F32, name=f"rest_ps{n}", tag=f"bank{rest_banks[n]}")
-            for i in range(1, PIECES):
-                second_layer(rest_ps[:, i - 1, :], n, i)
-            rest = keep.tile([P, J - PIECE], F32, name=f"rest{n}")
-            nc.scalar.copy(out=rest[:], in_=rest_ps[:].rearrange("p i j -> p (i j)"))
-            scatter(n, PIECE, J - PIECE, rest[:])
+            if n < 2:
+                result(n, PIECE, J - PIECE, PIECE, [7, 0][n])
+            else:
+                result(n, 0, J, J, n - 1)
             nc.sync.dma_start(out=out[n * P : (n + 1) * P, :], in_=windows[n][:])

from contextlib import ExitStack

import concourse.mybir as mybir
from concourse.masks import make_identity

K, T, J, N, L, R = 512, 1024, 512, 512, 512, 512
FLOPS = 2 * J * (K * R + R * N + L * N)

F32 = mybir.dt.float32
BF16 = mybir.dt.bfloat16
I32 = mybir.dt.int32
U32 = mybir.dt.uint32
U16 = mybir.dt.uint16
U8 = mybir.dt.uint8
FP8X4 = mybir.dt.float8_e4m3fn_x4
FP4X4 = mybir.dt.float4_e2m1fn_x4
RELU = mybir.ActivationFunctionType.Relu
COPY = mybir.ActivationFunctionType.Copy
MULT = mybir.AluOpType.mult

P = 128
PACK = 4
PIECE = 128
PIECES = J // PIECE
N_TILES = N // P
LIST_ROWS = 16


def load_scale_rows(queue, plane, scales, rows=range(4)):
    for b in rows:
        queue.dma_start(out=plane[b:P:32, :].bitcast(I32), in_=scales[0, b:16:4, :].bitcast(I32))


def tile_moe_expert_hidden_and_given_kernel(
    tc, xt_words, xt_scales, wa_words, wa_scales, wb_words, wb_scales, sx_words, sx_scales, wc_words, wc_scales, ga, offs, out
):
    nc = tc.nc

    def listed(window, first, count):
        return window.indirect(offsets[:, first // LIST_ROWS : (first + count) // LIST_ROWS])

    with ExitStack() as ctx:
        keep = ctx.enter_context(tc.tile_pool(name="keep", bufs=1))
        psum = ctx.enter_context(tc.psum_pool(name="psum", bufs=1))

        offsets = keep.tile([P, J // LIST_ROWS], U16, name="offsets")
        ga_cols = keep.tile([P, PACK], F32, name="ga_cols", tag="ga_cols", align_bytes=64)
        wa_raw = keep.tile([P, 2 * R], U8, name="wa_raw", align_bytes=64)
        wa_raw_scale = keep.tile([P, R], U8, name="wa_raw_scale", tag="wa_raw_scale", align_bytes=64)
        xt_w = keep.tile([P, T], I32, name="xt_w", tag="xt_w", align_bytes=64)
        xt_s = keep.tile([P, T], U8, name="xt_s", align_bytes=64)
        late_s = keep.tile([P, 3 * 512], U8, name="late_s", align_bytes=64)
        wb_s, wc_s, sx_s = late_s[:, 0:512], late_s[:, 512:1024], late_s[:, 1024:1536]
        ident = keep.tile([P, P], F32, name="ident", tag="ident", align_bytes=64)
        make_identity(nc, ident[:])
        windows = [keep.tile([P, T], F32, name=f"window{n}") for n in range(3)]

        nc.vector.memset(xt_s[:].bitcast(I32), 0)
        nc.vector.memset(wa_raw_scale[:].bitcast(I32), 0)
        nc.vector.memset(late_s[:].bitcast(I32), 0)
        nc.sync.dma_start(offsets[:], offs)
        nc.scalar.dma_start(out=wa_raw[:].bitcast(I32), in_=wa_words[0].bitcast(I32))
        nc.scalar.dma_start(out=ga_cols[:], in_=ga.rearrange("o (p c) -> (o p) c", c=PACK))
        load_scale_rows(nc.sync, xt_s, xt_scales, (0, 1))
        load_scale_rows(nc.scalar, xt_s, xt_scales, (2, 3))
        nc.sync.dma_start(out=xt_w[:], in_=xt_words[0].rearrange("p n t -> p (n t)").bitcast(I32))
        load_scale_rows(nc.scalar, wa_raw_scale, wa_scales, (0, 1))
        load_scale_rows(nc.sync, wa_raw_scale, wa_scales, (2, 3))

        late_w = keep.tile([P, 1280], I32, name="late_w", align_bytes=64)
        wb_w, wc_w, sx_w = late_w[:, 0:512], late_w[:, 512:1024], late_w[:, 1024:1280]
        load_scale_rows(nc.gpsimd, wb_s, wb_scales)
        nc.sync.dma_start(out=sx_w, in_=sx_words[0].bitcast(I32))
        nc.sync.dma_start(out=wc_w, in_=wc_words[0].rearrange("p n t -> p (n t)").bitcast(I32))
        load_scale_rows(nc.sync, sx_s, sx_scales, (0,))
        nc.sync.dma_start(out=wb_w, in_=wb_words[0].rearrange("p n t -> p (n t)").bitcast(I32))
        load_scale_rows(nc.sync, sx_s, sx_scales, (1, 2, 3))
        load_scale_rows(nc.sync, wc_s, wc_scales)

        for n in range(3):
            nc.vector.memset(windows[n][:].bitcast(I32), 0)

        gate_ps = psum.tile([P, PACK, P], F32, name="gate_ps", tag="bank0")
        for c in range(PACK):
            nc.tensor.transpose(gate_ps[:, c, :], ga_cols[:, c : c + 1].to_broadcast([P, P]), ident[:])
        gate = keep.tile([P, J], F32, name="gate")
        nc.scalar.activation(out=gate[:].rearrange("p (m c) -> p m c", c=PACK), in_=gate_ps[:].rearrange("p c m -> p m c"), func=COPY)

        wa_w = keep.tile([P, 2 * R], U8, name="wa_w", align_bytes=64)
        wa_s = keep.tile([P, R], U8, name="wa_s", tag="ident", align_bytes=64)
        nc.vector.tensor_copy(
            out=wa_w[:].bitcast(U16).rearrange("p (t m) -> p t m", t=PACK),
            in_=wa_raw[:].bitcast(U16).rearrange("p (m t) -> p t m", t=PACK),
        )

        def permute_scales():
            nc.vector.tensor_copy(
                out=wa_s[:].rearrange("p (t m) -> p t m", t=PACK),
                in_=wa_raw_scale[:].rearrange("p (m t) -> p t m", t=PACK),
            )

        def gather_words(dst, first, count):
            nc.vector.tensor_copy(dst, listed(xt_w[:].bitcast(U32), first, count))

        def gather_scales(dst, first, count):
            nc.vector.tensor_copy(dst, listed(xt_s[:], first, count))

        xg_s0 = keep.tile([P, PIECE], U8, name="xg_s0", align_bytes=64)
        xg_w0 = keep.tile([P, PIECE], U32, name="xg_w0", align_bytes=64)
        gather_scales(xg_s0[:], 0, PIECE)
        gather_words(xg_w0[:], 0, PIECE)
        permute_scales()
        xg_w123 = keep.tile([P, J - PIECE], U32, name="xg_w123", tag="wa_raw_scale", align_bytes=64)
        xg_s123 = keep.tile([P, J - PIECE], U8, name="xg_s123", tag="ga_cols", align_bytes=64)
        xg_w = [xg_w0[:]] + [xg_w123[:, i * PIECE : (i + 1) * PIECE] for i in range(PIECES - 1)]
        xg_s = [xg_s0[:]] + [xg_s123[:, i * PIECE : (i + 1) * PIECE] for i in range(PIECES - 1)]

        hid = [keep.tile([P, PIECE, PACK], BF16, name=f"hid{i}", tag=f"hid{i}", align_bytes=64) for i in range(PIECES)]
        hid_w = keep.tile([P, J], U32, name="hid_w", align_bytes=64)
        hid_s = keep.tile([P, J], U8, name="hid_s", align_bytes=64)
        a_ps = {}

        def first_layer(i, bank):
            a_ps[i] = psum.tile([P, PACK, PIECE], F32, name=f"a_ps{i}", tag=f"bank{bank}")
            for t in range(PACK):
                nc.tensor.matmul_mx(
                    out=a_ps[i][:, t, :],
                    lhsT=wa_w[:, 2 * P * t : 2 * P * (t + 1)].bitcast(FP4X4),
                    lhsT_scale=wa_s[:, P * t : P * (t + 1)],
                    rhs=xg_w[i].bitcast(FP8X4),
                    rhs_scale=xg_s[i],
                    start=True,
                    stop=True,
                )

        def relu(i):
            nc.scalar.activation(out=hid[i][:], in_=a_ps[i][:].rearrange("p t j -> p j t"), func=RELU)

        def quantize(i):
            cols = slice(i * PIECE, (i + 1) * PIECE)
            nc.vector.quantize_mx(out=hid_w[:, cols].bitcast(FP8X4), scales=hid_s[:, cols], in_=hid[i][:].rearrange("p j t -> p (j t)"))

        def second_layer(dst, n, first, count):
            rows = slice(n * P, (n + 1) * P)
            cols = slice(first, first + count)
            nc.tensor.matmul_mx(
                out=dst,
                lhsT=wc_w[:, rows].bitcast(FP8X4),
                lhsT_scale=wc_s[:, rows],
                rhs=sx_w[:, first // 2 : (first + count) // 2].bitcast(FP4X4),
                rhs_scale=sx_s[:, cols],
                start=True,
                stop=False,
            )
            nc.tensor.matmul_mx(
                out=dst,
                lhsT=wb_w[:, rows].bitcast(FP8X4),
                lhsT_scale=wb_s[:, rows],
                rhs=hid_w[:, cols].bitcast(FP8X4),
                rhs_scale=hid_s[:, cols],
                start=False,
                stop=True,
            )

        def scatter(n, first, count, src):
            nc.vector.tensor_tensor(listed(windows[n][:], first, count), src, gate[:, first : first + count], MULT)

        def result(n, first, count, step, bank):
            p_ps = psum.tile([P, count], F32, name=f"p_ps{n}_{first}", tag=f"bank{bank}")
            for j in range(0, count, step):
                second_layer(p_ps[:, j : j + step], n, first + j, step)
            p_sb = keep.tile([P, count], F32, name=f"p_sb{n}_{first}")
            nc.scalar.copy(out=p_sb[:], in_=p_ps[:])
            scatter(n, first, count, p_sb[:])
            return p_sb

        first_layer(0, 1)
        for i in range(1, PIECES):
            gather_words(xg_w[i], i * PIECE, PIECE)
            gather_scales(xg_s[i], i * PIECE, PIECE)
            first_layer(i, 1 + i)
        for i in range(PIECES):
            relu(i)
            quantize(i)
        windows.append(keep.tile([P, T], F32, name="window3", tag="xt_w", align_bytes=64))
        nc.vector.memset(windows[3][:].bitcast(I32), 0)

        lead0 = result(0, 0, PIECE, PIECE, 5)
        result(1, 0, PIECE, PIECE, 6)
        for n in range(N_TILES):
            if n < 2:
                result(n, PIECE, J - PIECE, PIECE, [7, 0][n])
            else:
                result(n, 0, J, J, n - 1)
            nc.sync.dma_start(out=out[n * P : (n + 1) * P, :], in_=windows[n][:])
